import numpy as np
import ml_dtypes


def mxq(x, axis, fmt="e4m3"):
    dtype, down = {"e4m3": (ml_dtypes.float8_e4m3fn, 7), "e5m2": (ml_dtypes.float8_e5m2, 14)}[fmt]
    v = np.moveaxis(np.asarray(x, np.float32).astype(ml_dtypes.bfloat16).astype(np.float64), axis, -1)
    blocks = v.reshape(v.shape[:-1] + (-1, 32))
    amax = np.abs(blocks).max(-1, keepdims=True)
    byte = np.maximum(np.where(amax > 0, np.frexp(amax)[1] - 1 + 127, 0) - down, 1)
    scale = np.exp2(byte - 127.0)
    codes = (blocks / scale).astype(np.float32).astype(dtype).astype(np.float64)
    return np.moveaxis((codes * scale).reshape(v.shape), -1, axis)


WIDE = False


def mx_kscale(k):
    if not WIDE:
        return np.ones(k)
    levels = np.array([10, -10, 5, -5, 0])
    if k % 512:
        return np.exp2(np.random.permutation(np.resize(levels, k // 32))).repeat(32)
    a = np.empty((k // 512, 16))
    for p in range(k // 512):
        a[p, :8] = np.random.permutation(np.resize(levels, 8))
        for g in range(8):
            far = levels[np.abs(levels - a[p, g]) >= 10]
            a[p, g + 8] = far[np.random.randint(len(far))]
    return np.exp2(a.ravel()).repeat(32)


def f64(x):
    return np.asarray(x).astype(np.float64)


def striped(idx):
    return np.tile(np.asarray(idx).reshape(-1, 16).T, (8, 1)).astype(np.uint16)


def unstriped(offs):
    return offs[:16].T.reshape(-1).astype(np.int64)


E2M1 = np.array([0.0, 0.5, 1.0, 1.5, 2.0, 3.0, 4.0, 6.0, -0.0, -0.5, -1.0, -1.5, -2.0, -3.0, -4.0, -6.0])


def pack_weight(w, fmt):
    k, n = w.shape
    w = f64(np.asarray(w, np.float32).astype(ml_dtypes.bfloat16)).reshape(k // 32, 32, n)
    amax = np.abs(w).max(1)
    if fmt == "e4m3":
        byte = np.frexp(amax)[1] - 1 + 127 - 7
    else:
        mant, ex = np.frexp(amax / 6.0)
        byte = np.where(mant > 0.5, ex, ex - 1) + 127
    byte = np.clip(np.where(amax > 0, byte, 1), 1, 254)
    scaled = (w * np.exp2(127.0 - byte)[:, None, :]).reshape(k, n).astype(np.float32)
    by_word = np.ascontiguousarray(scaled.reshape(k // 512, 128, 4, n).transpose(0, 1, 3, 2))
    if fmt == "e4m3":
        words = by_word.astype(ml_dtypes.float8_e4m3fn).view(np.uint8)
    else:
        c = by_word.astype(ml_dtypes.float4_e2m1fn).view(np.uint8) & 0xF
        words = (c[..., 0::2] | (c[..., 1::2] << 4)).reshape(k // 512, 128, 2 * n)
    return np.ascontiguousarray(words), np.ascontiguousarray(byte.astype(np.uint8).reshape(k // 512, 16, n))


def unpack_weight(words, scales, fmt):
    g, _, n = scales.shape
    words = np.ascontiguousarray(words).reshape(g, 128, n, -1)
    if fmt == "e4m3":
        vals = words.view(ml_dtypes.float8_e4m3fn).astype(np.float64)
    else:
        nib = np.empty((g, 128, n, 4), np.uint8)
        nib[..., 0::2] = words & 0xF
        nib[..., 1::2] = words >> 4
        vals = E2M1[nib]
    vals = vals * np.repeat(np.exp2(scales.astype(np.float64) - 127.0), 8, axis=1)[..., None]
    return vals.transpose(0, 1, 3, 2).reshape(g * 512, n)


def sigmoid(v):
    return 1.0 / (1.0 + np.exp(-v))


D, E, T, I, Q = 512, 512, 2048, 512, 128


def setup_inputs():
    n = np.random.standard_normal
    idx = np.random.permutation(T)[:I]
    fd = mx_kscale(D)
    fi = mx_kscale(I)
    ti = np.ones(T)
    ti[idx] = fi
    keysp = pack_weight(n((D, T)) / fd[:, None], "e4m3")
    return {
        "query": (n((D, Q)) * 0.8 / np.sqrt(D) * fd[:, None]).astype(np.float32),
        "keys_words": keysp[0],
        "keys_scales": keysp[1],
        "share": (np.random.uniform(0.2, 0.8, (Q, 1))).astype(np.float32),
        "dquery": (n((D, Q)) * 0.6 / np.sqrt(D) * fd[:, None]).astype(np.float32),
        "os": (np.random.uniform(4.0, 16.0, (1, I)) * fi).astype(np.float32),
        "vals": (n((E, T)) / ti).astype(np.float32),
        "offs": striped(idx),
    }


def reference(query, keys_words, keys_scales, share, dquery, os, vals, offs):
    idx = unstriped(offs)
    keysu = unpack_weight(keys_words, keys_scales, "e4m3")
    queryq = mxq(f64(query), 0, "e4m3")
    keysidxg = keysu[:, idx]
    a = queryq.T @ keysidxg
    dqueryq = mxq(f64(dquery), 0, "e4m3")
    ta = dqueryq.T @ keysidxg
    e0 = np.exp(a)
    s0 = sigmoid(a)
    p = e0 * f64(share) + s0 * (1.0 - f64(share)) * 3.0
    z = np.sum(p, axis=1, keepdims=True)
    te0 = ta * e0
    ts0 = ta * s0 * (1.0 - s0)
    tp = te0 * f64(share) + ts0 * (1.0 - f64(share)) * 3.0
    tz = np.sum(tp, axis=1, keepdims=True)
    tw = (tp - tz * p / z) / z
    wo1 = tw * f64(os)
    wt1 = wo1.T
    vt1 = f64(vals)[:, idx].T
    wt1q = mxq(wt1, 0, "e4m3")
    vt1q = mxq(vt1, 0, "e4m3")
    o = wt1q.T @ vt1q
    return o

@@ -1,0 +1,182 @@
+from contextlib import ExitStack
+
+import concourse.mybir as mybir
+from concourse.masks import make_identity
+
+D, E, T, I, Q = 512, 512, 2048, 512, 128
+FLOPS = 2 * D * Q * I * 2 + 2 * I * Q * E
+
+F32 = mybir.dt.float32
+BF16 = mybir.dt.bfloat16
+I32 = mybir.dt.int32
+U32 = mybir.dt.uint32
+U16 = mybir.dt.uint16
+U8 = mybir.dt.uint8
+FP8X4 = mybir.dt.float8_e4m3fn_x4
+ALU = mybir.AluOpType
+ACT = mybir.ActivationFunctionType
+
+P = 128
+PACK = 4
+CHUNKS = E // P
+
+
+def tile_attend_ttmixedparts_kernel(tc, query, keys_words, keys_scales, share, dquery, slot_factor, vals, offs, out):
+    nc = tc.nc
+    with ExitStack() as ctx:
+        sb = ctx.enter_context(tc.tile_pool(name="sb", bufs=1))
+        ps = ctx.enter_context(tc.psum_pool(name="ps", bufs=1))
+
+        offsets = sb.tile([P, I // 16], U16, name="offsets")
+        nc.sync.dma_start(offsets[:], offs)
+
+        key_scales = sb.tile([P, T], U8, name="key_scales")
+        nc.vector.memset(key_scales[:].bitcast(I32), 0)
+        for quad in range(4):
+            nc.scalar.dma_start(
+                out=key_scales[32 * quad : 32 * quad + 4, :].bitcast(I32),
+                in_=keys_scales[0, 4 * quad : 4 * quad + 4, :].bitcast(I32),
+            )
+
+        q_raw = sb.tile([P, PACK, Q], F32, name="q_raw")
+        nc.sync.dma_start(out=q_raw[:], in_=query.rearrange("(p j) q -> p j q", j=PACK))
+        key_words = sb.tile([P, T], U32, name="key_words")
+        nc.sync.dma_start(out=key_words[:].bitcast(I32), in_=keys_words[0].rearrange("p n t -> p (n t)").bitcast(I32))
+        share_col = sb.tile([P, 1], F32, name="share_col")
+        nc.scalar.dma_start(out=share_col[:], in_=share)
+        os_slots = sb.tile([P, PACK], F32, name="os_slots")
+        nc.scalar.dma_start(out=os_slots[:], in_=slot_factor.rearrange("o (p t) -> (o p) t", t=PACK))
+
+        val_pool = [sb.tile([P, T], F32, name="val_pool%d" % c) for c in range(CHUNKS)]
+        dq_raw = sb.tile([P, PACK, Q], F32, name="dq_raw")
+        nc.sync.dma_start(out=val_pool[0][:], in_=vals[0:P, :])
+        nc.sync.dma_start(out=dq_raw[:], in_=dquery.rearrange("(p j) q -> p j q", j=PACK))
+        for c in range(1, CHUNKS):
+            nc.sync.dma_start(out=val_pool[c][:], in_=vals[c * P : (c + 1) * P, :])
+
+        ident = sb.tile([P, P], F32, name="ident")
+        make_identity(nc, ident[:])
+        half = sb.tile([P, 1], F32, name="half")
+        nc.gpsimd.memset(half[:], 0.5)
+        warm = sb.tile([P, 1], F32, name="warm")
+        nc.scalar.activation(out=warm[:], in_=half[:], func=ACT.Exp)
+
+        mix = sb.tile([P, 2], F32, name="mix")
+        nc.scalar.activation(out=mix[:, 0:1], in_=share_col[:], func=ACT.Copy, scale=-1.5, bias=1.5)
+        nc.scalar.activation(out=mix[:, 1:2], in_=share_col[:], func=ACT.Copy, scale=3.0, bias=-3.0)
+
+        k_scales = sb.tile([P, I], U8, name="k_scales", align_bytes=64)
+        nc.vector.tensor_copy(out=k_scales[:], in_=key_scales[:].indirect(offsets[:]))
+        q_bf = sb.tile([P, Q, PACK], BF16, name="q_bf", align_bytes=64)
+        nc.vector.tensor_copy(out=q_bf[:], in_=q_raw[:].rearrange("p j q -> p q j"))
+        q_codes = sb.tile([P, Q], U32, name="q_codes", align_bytes=64)
+        q_scales = sb.tile([P, Q], U8, name="q_scales", align_bytes=64)
+        nc.vector.quantize_mx(out=q_codes[:].bitcast(FP8X4), scales=q_scales[:], in_=q_bf[:].rearrange("p q j -> p (q j)"))
+        k_codes = sb.tile([P, I], U32, name="k_codes", align_bytes=64)
+        nc.vector.tensor_copy(out=k_codes[:], in_=key_words[:].indirect(offsets[:]))
+
+        a_ps = ps.tile([P, I], F32, name="a_ps")
+        nc.tensor.matmul_mx(out=a_ps[:], lhsT=q_codes[:].bitcast(FP8X4), lhsT_scale=q_scales[:],
+                            rhs=k_codes[:].bitcast(FP8X4), rhs_scale=k_scales[:], start=True, stop=True)
+        a_dealt = a_ps[:].rearrange("q (p t) -> q t p", t=PACK)
+
+        row_max = sb.tile([P, 1], F32, name="row_max")
+        nc.vector.tensor_reduce(out=row_max[:], in_=a_ps[:], axis=mybir.AxisListType.X, op=ALU.max, negate=True)
+        shift = sb.tile([P, 1], F32, name="shift")
+        nc.vector.tensor_scalar(out=shift[:], in0=row_max[:], scalar1=0.0, scalar2=None, op0=ALU.min)
+        e = sb.tile([P, PACK, P], F32, name="e")
+        nc.scalar.activation(out=e[:], in_=a_dealt, func=ACT.Exp, bias=shift[:])
+        shrink = sb.tile([P, 1], F32, name="shrink")
+        nc.scalar.activation(out=shrink[:], in_=shift[:], func=ACT.Exp)
+        mix_s = sb.tile([P, 2], F32, name="mix_s")
+        nc.scalar.activation(out=mix_s[:], in_=mix[:], func=ACT.Copy, scale=shrink[:])
+        u = sb.tile([P, PACK, P], F32, name="u")
+        nc.scalar.activation(out=u[:], in_=a_dealt, func=ACT.Tanh, scale=0.5)
+        s_sq = sb.tile([P, I], F32, name="s_sq")
+        nc.scalar.activation(out=s_sq[:], in_=u[:].rearrange("q t p -> q (t p)"), func=ACT.Square, scale=0.5, bias=half[:])
+
+        v_codes = sb.tile([P, E], U32, name="v_codes", align_bytes=64)
+        v_scales = sb.tile([P, E], U8, name="v_scales", align_bytes=64)
+
+        def gather_values(c):
+            picked = sb.tile([P, I], BF16, name="picked%d" % c)
+            nc.vector.tensor_copy(out=picked[:], in_=val_pool[c][:].indirect(offsets[:]))
+            words = picked[:].bitcast(F32)
+            turned = ps.tile([P, 2, P], F32, name="turned", tag="turned", bufs=2)
+            for h in range(2):
+                nc.tensor.transpose(turned[:, h, :], words[:, h : I // 2 : 2], ident[:])
+            v_bf = sb.tile([P, P, PACK], BF16, name="v_bf%d" % c, align_bytes=64)
+            nc.scalar.copy(out=v_bf[:].rearrange("p e t -> p (e t)").bitcast(F32).rearrange("p (e h) -> p e h", h=2),
+                           in_=turned[:].rearrange("p h e -> p e h"))
+            return v_bf
+
+        def quantize_values(c, v_bf):
+            cols = slice(c * P, (c + 1) * P)
+            nc.vector.quantize_mx(out=v_codes[:, cols].bitcast(FP8X4), scales=v_scales[:, cols],
+                                  in_=v_bf[:].rearrange("p e t -> p (e t)"))
+
+        v0 = gather_values(0)
+
+        dq_bf = sb.tile([P, Q, PACK], BF16, name="dq_bf", align_bytes=64)
+        nc.scalar.copy(out=dq_bf[:], in_=dq_raw[:].rearrange("p j q -> p q j"))
+        dq_codes = sb.tile([P, Q], U32, name="dq_codes", align_bytes=64)
+        dq_scales = sb.tile([P, Q], U8, name="dq_scales", align_bytes=64)
+        nc.vector.quantize_mx(out=dq_codes[:].bitcast(FP8X4), scales=dq_scales[:], in_=dq_bf[:].rearrange("p q j -> p (q j)"))
+        ta_ps = ps.tile([P, I], F32, name="ta_ps")
+        nc.tensor.matmul_mx(out=ta_ps[:], lhsT=dq_codes[:].bitcast(FP8X4), lhsT_scale=dq_scales[:],
+                            rhs=k_codes[:].bitcast(FP8X4), rhs_scale=k_scales[:], start=True, stop=True)
+        ta_dealt = ta_ps[:].rearrange("q (p t) -> q t p", t=PACK)
+
+        base = sb.tile([P, I], F32, name="base")
+        nc.vector.tensor_scalar(out=base[:], in0=e[:].rearrange("q t p -> q (t p)"), scalar1=share_col[:], scalar2=mix_s[:, 0:1],
+                                op0=ALU.mult, op1=ALU.add)
+        part = sb.tile([P, I], F32, name="part")
+        z = sb.tile([P, 1], F32, name="z")
+        nc.vector.scalar_tensor_tensor(out=part[:], in0=u[:].rearrange("q t p -> q (t p)"), scalar=mix_s[:, 0:1], in1=base[:],
+                                       op0=ALU.mult, op1=ALU.add, accum_out=z[:])
+        slope = sb.tile([P, I], F32, name="slope")
+        nc.vector.scalar_tensor_tensor(out=slope[:], in0=s_sq[:], scalar=mix_s[:, 1:2], in1=part[:], op0=ALU.mult, op1=ALU.add)
+        z_inv = sb.tile([P, 1], F32, name="z_inv")
+        nc.vector.reciprocal(out=z_inv[:], in_=z[:])
+        weight = sb.tile([P, I], F32, name="weight")
+        nc.scalar.activation(out=weight[:], in_=part[:], func=ACT.Copy, scale=z_inv[:])
+        tpz = sb.tile([P, PACK, P], F32, name="tpz")
+        ratio = sb.tile([P, 1], F32, name="ratio")
+        nc.vector.scalar_tensor_tensor(out=tpz[:], in0=slope[:].rearrange("q (t p) -> q t p", t=PACK), scalar=z_inv[:], in1=ta_dealt,
+                                       op0=ALU.mult, op1=ALU.mult, accum_out=ratio[:])
+        quantize_values(0, v0)
+        v1 = gather_values(1)
+        neg_tw = sb.tile([P, I], F32, name="neg_tw")
+        nc.vector.scalar_tensor_tensor(out=neg_tw[:], in0=weight[:], scalar=ratio[:], in1=tpz[:].rearrange("q t p -> q (t p)"),
+                                       op0=ALU.mult, op1=ALU.subtract)
+        tw_ps = ps.tile([P, PACK, Q], F32, name="tw_ps")
+        for t in range(PACK):
+            nc.tensor.transpose(tw_ps[:, t, :], neg_tw[:, t * P : (t + 1) * P], ident[:])
+        quantize_values(1, v1)
+        v2 = gather_values(2)
+        w_bf = sb.tile([P, Q, PACK], BF16, name="w_bf", align_bytes=64)
+        nc.vector.scalar_tensor_tensor(out=w_bf[:], in0=tw_ps[:].rearrange("p t q -> p q t"), scalar=-1.0,
+                                       in1=os_slots[:].unsqueeze(1).to_broadcast([P, Q, PACK]), op0=ALU.mult, op1=ALU.mult)
+        quantize_values(2, v2)
+        w_codes = sb.tile([P, Q], U32, name="w_codes", align_bytes=64)
+        w_scales = sb.tile([P, Q], U8, name="w_scales", align_bytes=64)
+        nc.vector.quantize_mx(out=w_codes[:].bitcast(FP8X4), scales=w_scales[:], in_=w_bf[:].rearrange("p q t -> p (q t)"))
+        v3 = gather_values(3)
+        quantize_values(3, v3)
+
+        def product(bank, first, width):
+            cols = slice(first, first + width)
+            nc.tensor.matmul_mx(out=bank, lhsT=w_codes[:].bitcast(FP8X4), lhsT_scale=w_scales[:],
+                                rhs=v_codes[:, cols].bitcast(FP8X4), rhs_scale=v_scales[:, cols], start=True, stop=True)
+
+        early_ps = ps.tile([P, 3 * P], F32, name="early_ps")
+        product(early_ps[:, 0 : 2 * P], 0, 2 * P)
+        product(early_ps[:, 2 * P : 3 * P], 2 * P, P)
+        early = sb.tile([P, 3 * P], F32, name="early")
+        nc.scalar.copy(out=early[:], in_=early_ps[:])
+        nc.sync.dma_start(out=out[:, 0 : 3 * P], in_=early[:])
+        late_ps = ps.tile([P, P], F32, name="late_ps")
+        product(late_ps[:], 3 * P, P)
+        late = sb.tile([P, P], F32, name="late")
+        nc.vector.tensor_copy(out=late[:], in_=late_ps[:])
+        nc.sync.dma_start(out=out[:, 3 * P : E], in_=late[:])

@@ -30,40 +30,46 @@ def tile_attend_ttmixedparts_kernel(tc, query, keys_words, keys_scales, share, d
         offsets = sb.tile([P, I // 16], U16, name="offsets")
         nc.sync.dma_start(offsets[:], offs)
 
+        q_raw = sb.tile([P, PACK, Q], F32, name="q_raw")
+        nc.sync.dma_start(out=q_raw[:], in_=query.rearrange("(p j) q -> p j q", j=PACK))
         key_scales = sb.tile([P, T], U8, name="key_scales")
-        nc.vector.memset(key_scales[:].bitcast(I32), 0)
+        nc.gpsimd.memset(key_scales[:].bitcast(I32), 0)
         for quad in range(4):
-            nc.scalar.dma_start(
+            nc.sync.dma_start(
                 out=key_scales[32 * quad : 32 * quad + 4, :].bitcast(I32),
                 in_=keys_scales[0, 4 * quad : 4 * quad + 4, :].bitcast(I32),
             )
 
-        q_raw = sb.tile([P, PACK, Q], F32, name="q_raw")
-        nc.sync.dma_start(out=q_raw[:], in_=query.rearrange("(p j) q -> p j q", j=PACK))
         key_words = sb.tile([P, T], U32, name="key_words")
         nc.sync.dma_start(out=key_words[:].bitcast(I32), in_=keys_words[0].rearrange("p n t -> p (n t)").bitcast(I32))
-        share_col = sb.tile([P, 1], F32, name="share_col")
-        nc.scalar.dma_start(out=share_col[:], in_=share)
-        os_slots = sb.tile([P, PACK], F32, name="os_slots")
-        nc.scalar.dma_start(out=os_slots[:], in_=slot_factor.rearrange("o (p t) -> (o p) t", t=PACK))
-
-        val_pool = [sb.tile([P, T], F32, name="val_pool%d" % c) for c in range(CHUNKS)]
         dq_raw = sb.tile([P, PACK, Q], F32, name="dq_raw")
-        nc.sync.dma_start(out=val_pool[0][:], in_=vals[0:P, :])
         nc.sync.dma_start(out=dq_raw[:], in_=dquery.rearrange("(p j) q -> p j q", j=PACK))
+        share_col = sb.tile([P, 1], F32, name="share_col")
+        nc.sync.dma_start(out=share_col[:], in_=share)
+        os_slots = sb.tile([P, PACK], F32, name="os_slots")
+        nc.sync.dma_start(out=os_slots[:], in_=slot_factor.rearrange("o (p t) -> (o p) t", t=PACK))
+
+        val_pool = [sb.tile([P, T], F32, name="val_pool%d" % c, tag="pool%d" % c, align_bytes=64) for c in range(CHUNKS)]
+        nc.sync.dma_start(out=val_pool[0][:], in_=vals[0:P, :])
         for c in range(1, CHUNKS):
             nc.sync.dma_start(out=val_pool[c][:], in_=vals[c * P : (c + 1) * P, :])
 
         ident = sb.tile([P, P], F32, name="ident")
         make_identity(nc, ident[:])
-        half = sb.tile([P, 1], F32, name="half")
-        nc.gpsimd.memset(half[:], 0.5)
+        zero = sb.tile([P, 1], F32, name="zero")
+        nc.gpsimd.memset(zero[:], 0.0)
+        multiples = sb.tile([P, 5], F32, name="multiples")
+        for col, value in enumerate((-0.5, -0.25, 0.25, 0.5, I / 2)):
+            nc.gpsimd.memset(multiples[:, col : col + 1], value)
+        mix_s = sb.tile([P, 6], F32, name="mix_s")
+        nc.gpsimd.memset(mix_s[:, 0:1], -1.0)
         warm = sb.tile([P, 1], F32, name="warm")
-        nc.scalar.activation(out=warm[:], in_=half[:], func=ACT.Exp)
+        nc.scalar.activation(out=warm[:], in_=zero[:], func=ACT.Exp)
 
-        mix = sb.tile([P, 2], F32, name="mix")
-        nc.scalar.activation(out=mix[:, 0:1], in_=share_col[:], func=ACT.Copy, scale=-1.5, bias=1.5)
-        nc.scalar.activation(out=mix[:, 1:2], in_=share_col[:], func=ACT.Copy, scale=3.0, bias=-3.0)
+        rest = sb.tile([P, 1], F32, name="rest")
+        nc.scalar.activation(out=rest[:], in_=share_col[:], func=ACT.Copy, scale=-3.0, bias=3.0)
+        mix = sb.tile([P, 5], F32, name="mix")
+        nc.scalar.activation(out=mix[:], in_=multiples[:], func=ACT.Copy, scale=rest[:])
 
         k_scales = sb.tile([P, I], U8, name="k_scales", align_bytes=64)
         nc.vector.tensor_copy(out=k_scales[:], in_=key_scales[:].indirect(offsets[:]))
@@ -73,49 +79,20 @@ def tile_attend_ttmixedparts_kernel(tc, query, keys_words, keys_scales, share, d
         q_scales = sb.tile([P, Q], U8, name="q_scales", align_bytes=64)
         nc.vector.quantize_mx(out=q_codes[:].bitcast(FP8X4), scales=q_scales[:], in_=q_bf[:].rearrange("p q j -> p (q j)"))
         k_codes = sb.tile([P, I], U32, name="k_codes", align_bytes=64)
-        nc.vector.tensor_copy(out=k_codes[:], in_=key_words[:].indirect(offsets[:]))
-
-        a_ps = ps.tile([P, I], F32, name="a_ps")
-        nc.tensor.matmul_mx(out=a_ps[:], lhsT=q_codes[:].bitcast(FP8X4), lhsT_scale=q_scales[:],
-                            rhs=k_codes[:].bitcast(FP8X4), rhs_scale=k_scales[:], start=True, stop=True)
-        a_dealt = a_ps[:].rearrange("q (p t) -> q t p", t=PACK)
-
-        row_max = sb.tile([P, 1], F32, name="row_max")
-        nc.vector.tensor_reduce(out=row_max[:], in_=a_ps[:], axis=mybir.AxisListType.X, op=ALU.max, negate=True)
-        shift = sb.tile([P, 1], F32, name="shift")
-        nc.vector.tensor_scalar(out=shift[:], in0=row_max[:], scalar1=0.0, scalar2=None, op0=ALU.min)
-        e = sb.tile([P, PACK, P], F32, name="e")
-        nc.scalar.activation(out=e[:], in_=a_dealt, func=ACT.Exp, bias=shift[:])
-        shrink = sb.tile([P, 1], F32, name="shrink")
-        nc.scalar.activation(out=shrink[:], in_=shift[:], func=ACT.Exp)
-        mix_s = sb.tile([P, 2], F32, name="mix_s")
-        nc.scalar.activation(out=mix_s[:], in_=mix[:], func=ACT.Copy, scale=shrink[:])
-        u = sb.tile([P, PACK, P], F32, name="u")
-        nc.scalar.activation(out=u[:], in_=a_dealt, func=ACT.Tanh, scale=0.5)
-        s_sq = sb.tile([P, I], F32, name="s_sq")
-        nc.scalar.activation(out=s_sq[:], in_=u[:].rearrange("q t p -> q (t p)"), func=ACT.Square, scale=0.5, bias=half[:])
-
-        v_codes = sb.tile([P, E], U32, name="v_codes", align_bytes=64)
-        v_scales = sb.tile([P, E], U8, name="v_scales", align_bytes=64)
-
-        def gather_values(c):
-            picked = sb.tile([P, I], BF16, name="picked%d" % c)
-            nc.vector.tensor_copy(out=picked[:], in_=val_pool[c][:].indirect(offsets[:]))
-            words = picked[:].bitcast(F32)
-            turned = ps.tile([P, 2, P], F32, name="turned", tag="turned", bufs=2)
-            for h in range(2):
-                nc.tensor.transpose(turned[:, h, :], words[:, h : I // 2 : 2], ident[:])
-            v_bf = sb.tile([P, P, PACK], BF16, name="v_bf%d" % c, align_bytes=64)
-            nc.scalar.copy(out=v_bf[:].rearrange("p e t -> p (e t)").bitcast(F32).rearrange("p (e h) -> p e h", h=2),
-                           in_=turned[:].rearrange("p h e -> p e h"))
-            return v_bf
-
-        def quantize_values(c, v_bf):
-            cols = slice(c * P, (c + 1) * P)
-            nc.vector.quantize_mx(out=v_codes[:, cols].bitcast(FP8X4), scales=v_scales[:, cols],
-                                  in_=v_bf[:].rearrange("p e t -> p (e t)"))
-
-        v0 = gather_values(0)
+        neg_a = sb.tile([P, PACK, P], F32, name="neg_a")
+        shift_so_far = zero
+        for h in range(2):
+            slots = slice(h * I // 2, (h + 1) * I // 2)
+            nc.vector.tensor_copy(out=k_codes[:, slots], in_=key_words[:].indirect(offsets[:, h * I // 32 : (h + 1) * I // 32]))
+        for h in range(2):
+            slots = slice(h * I // 2, (h + 1) * I // 2)
+            a_ps = ps.tile([P, I // 2], F32, name="a_ps%d" % h)
+            nc.tensor.matmul_mx(out=a_ps[:], lhsT=q_codes[:].bitcast(FP8X4), lhsT_scale=q_scales[:],
+                                rhs=k_codes[:, slots].bitcast(FP8X4), rhs_scale=k_scales[:, slots], start=True, stop=True)
+            shift = sb.tile([P, 1], F32, name="shift%d" % h, tag=("hold0", "shift")[h], align_bytes=64)
+            nc.vector.tensor_scalar(out=neg_a[:, :, h * P // 2 : (h + 1) * P // 2], in0=a_ps[:].rearrange("q (p t) -> q t p", t=PACK),
+                                    scalar1=-1.0, scalar2=shift_so_far[:], op0=ALU.mult, op1=ALU.min, accum_out=shift[:])
+            shift_so_far = shift
 
         dq_bf = sb.tile([P, Q, PACK], BF16, name="dq_bf", align_bytes=64)
         nc.scalar.copy(out=dq_bf[:], in_=dq_raw[:].rearrange("p j q -> p q j"))
@@ -127,56 +104,95 @@ def tile_attend_ttmixedparts_kernel(tc, query, keys_words, keys_scales, share, d
                             rhs=k_codes[:].bitcast(FP8X4), rhs_scale=k_scales[:], start=True, stop=True)
         ta_dealt = ta_ps[:].rearrange("q (p t) -> q t p", t=PACK)
 
-        base = sb.tile([P, I], F32, name="base")
-        nc.vector.tensor_scalar(out=base[:], in0=e[:].rearrange("q t p -> q (t p)"), scalar1=share_col[:], scalar2=mix_s[:, 0:1],
-                                op0=ALU.mult, op1=ALU.add)
-        part = sb.tile([P, I], F32, name="part")
+        neg_flat = neg_a[:].rearrange("q t p -> q (t p)")
+        u = sb.tile([P, I], F32, name="u")
+        u_sum = sb.tile([P, 1], F32, name="u_sum")
+        nc.scalar.activation(out=u[:], in_=neg_flat, func=ACT.Tanh, scale=-0.5, accum_out=u_sum[:])
+        shrink = sb.tile([P, 1], F32, name="shrink")
+        nc.scalar.activation(out=shrink[:], in_=shift[:], func=ACT.Exp)
+        e = sb.tile([P, I], F32, name="e", tag="hold5", align_bytes=64)
+        e_sum = sb.tile([P, 1], F32, name="e_sum")
+        nc.scalar.activation(out=e[:], in_=neg_flat, func=ACT.Exp, scale=-1.0, bias=shift[:], accum_out=e_sum[:])
+        nc.scalar.activation(out=mix_s[:, 1:6], in_=mix[:], func=ACT.Copy, scale=shrink[:])
+        s_sum = sb.tile([P, 1], F32, name="s_sum")
+        nc.scalar.activation(out=s_sum[:], in_=u_sum[:], func=ACT.Identity, scale=mix_s[:, 4:5], bias=mix_s[:, 5:6])
         z = sb.tile([P, 1], F32, name="z")
-        nc.vector.scalar_tensor_tensor(out=part[:], in0=u[:].rearrange("q t p -> q (t p)"), scalar=mix_s[:, 0:1], in1=base[:],
-                                       op0=ALU.mult, op1=ALU.add, accum_out=z[:])
-        slope = sb.tile([P, I], F32, name="slope")
-        nc.vector.scalar_tensor_tensor(out=slope[:], in0=s_sq[:], scalar=mix_s[:, 1:2], in1=part[:], op0=ALU.mult, op1=ALU.add)
-        z_inv = sb.tile([P, 1], F32, name="z_inv")
+        nc.scalar.activation(out=z[:], in_=e_sum[:], func=ACT.Identity, scale=share_col[:], bias=s_sum[:])
+
+        def gather_values(c):
+            picked = sb.tile([P, I], BF16, name="picked%d" % c, tag=("hold0", "hold1", "hold3", "pool2")[c], align_bytes=64)
+            nc.vector.tensor_copy(out=picked[:], in_=val_pool[c][:].indirect(offsets[:]))
+            words = picked[:].bitcast(F32)
+            turned = ps.tile([P, 2, P], F32, name="turned", tag="turned", bufs=3)
+            for h in range(2):
+                nc.tensor.transpose(turned[:, h, :], words[:, h : I // 2 : 2], ident[:])
+            return turned
+
+        def interleave(turned, rows):
+            nc.scalar.copy(out=rows.bitcast(F32).rearrange("p (e h) -> p e h", h=2), in_=turned[:].rearrange("p h e -> p e h"))
+
+        def quantize(codes, scales, rows):
+            nc.vector.quantize_mx(out=codes.bitcast(FP8X4), scales=scales, in_=rows)
+
+        turned0 = gather_values(0)
+        u_sq = sb.tile([P, I], F32, name="u_sq", tag="pool0", align_bytes=64)
+        nc.vector.tensor_tensor(out=u_sq[:], in0=u[:], in1=u[:], op=ALU.mult)
+        base = sb.tile([P, I], F32, name="base")
+        nc.vector.tensor_scalar(out=base[:], in0=e[:], scalar1=share_col[:], scalar2=mix_s[:, 3:4], op0=ALU.mult, op1=ALU.add)
+        z_inv = sb.tile([P, 1], F32, name="z_inv", tag="hold3", align_bytes=64)
         nc.vector.reciprocal(out=z_inv[:], in_=z[:])
-        weight = sb.tile([P, I], F32, name="weight")
-        nc.scalar.activation(out=weight[:], in_=part[:], func=ACT.Copy, scale=z_inv[:])
-        tpz = sb.tile([P, PACK, P], F32, name="tpz")
+        slope = sb.tile([P, I], F32, name="slope", tag="hold1", align_bytes=64)
+        nc.vector.scalar_tensor_tensor(out=slope[:], in0=u_sq[:], scalar=mix_s[:, 2:3], in1=base[:], op0=ALU.mult, op1=ALU.add)
+        v0 = sb.tile([P, I], BF16, name="v0", tag="hold5", align_bytes=64)
+        interleave(turned0, v0[:])
+        per_z = sb.tile([P, 3], F32, name="per_z")
+        nc.scalar.activation(out=per_z[:], in_=mix_s[:, 0:3], func=ACT.Copy, scale=z_inv[:])
+        terms = [sb.tile([P, PACK, P], F32, name="term%d" % n) for n in range(3)]
         ratio = sb.tile([P, 1], F32, name="ratio")
-        nc.vector.scalar_tensor_tensor(out=tpz[:], in0=slope[:].rearrange("q (t p) -> q t p", t=PACK), scalar=z_inv[:], in1=ta_dealt,
+        nc.vector.scalar_tensor_tensor(out=terms[0][:], in0=slope[:].rearrange("q (t p) -> q t p", t=PACK), scalar=z_inv[:], in1=ta_dealt,
                                        op0=ALU.mult, op1=ALU.mult, accum_out=ratio[:])
-        quantize_values(0, v0)
-        v1 = gather_values(1)
-        neg_tw = sb.tile([P, I], F32, name="neg_tw")
-        nc.vector.scalar_tensor_tensor(out=neg_tw[:], in0=weight[:], scalar=ratio[:], in1=tpz[:].rearrange("q t p -> q (t p)"),
-                                       op0=ALU.mult, op1=ALU.subtract)
+        pull = sb.tile([P, 3], F32, name="pull")
+        nc.scalar.activation(out=pull[:], in_=per_z[:], func=ACT.Copy, scale=ratio[:])
+        nc.scalar.activation(out=terms[1][:].rearrange("q t p -> q (t p)"), in_=base[:], func=ACT.Copy, scale=pull[:, 0:1])
+        nc.scalar.activation(out=terms[2][:].rearrange("q t p -> q (t p)"), in_=u[:], func=ACT.Identity, scale=pull[:, 1:2], bias=pull[:, 2:3])
         tw_ps = ps.tile([P, PACK, Q], F32, name="tw_ps")
-        for t in range(PACK):
-            nc.tensor.transpose(tw_ps[:, t, :], neg_tw[:, t * P : (t + 1) * P], ident[:])
-        quantize_values(1, v1)
-        v2 = gather_values(2)
-        w_bf = sb.tile([P, Q, PACK], BF16, name="w_bf", align_bytes=64)
-        nc.vector.scalar_tensor_tensor(out=w_bf[:], in0=tw_ps[:].rearrange("p t q -> p q t"), scalar=-1.0,
-                                       in1=os_slots[:].unsqueeze(1).to_broadcast([P, Q, PACK]), op0=ALU.mult, op1=ALU.mult)
-        quantize_values(2, v2)
-        w_codes = sb.tile([P, Q], U32, name="w_codes", align_bytes=64)
-        w_scales = sb.tile([P, Q], U8, name="w_scales", align_bytes=64)
-        nc.vector.quantize_mx(out=w_codes[:].bitcast(FP8X4), scales=w_scales[:], in_=w_bf[:].rearrange("p q t -> p (q t)"))
-        v3 = gather_values(3)
-        quantize_values(3, v3)
+        for n, term in enumerate(terms):
+            for t in range(PACK):
+                nc.tensor.matmul(tw_ps[:, t, :], lhsT=term[:, t, :], rhs=ident[:], is_transpose=True,
+                                 start=(n == 0 and t == 0), stop=(n == len(terms) - 1 and t == PACK - 1))
+        turned1 = gather_values(1)
+        turned2 = gather_values(2)
+        v0_codes = sb.tile([P, P], U32, name="v0_codes", tag="pool1", align_bytes=64)
+        v0_scales = sb.tile([P, P], U8, name="v0_scales", align_bytes=64)
+        quantize(v0_codes[:], v0_scales[:], v0[:])
+        turned3 = gather_values(3)
+        wv = sb.tile([P, 3 * I], BF16, name="wv", tag="pool3", align_bytes=64)
+        nc.vector.tensor_tensor(out=wv[:, 0:I].rearrange("p (q t) -> p q t", t=PACK), in0=tw_ps[:].rearrange("p t q -> p q t"),
+                                in1=os_slots[:].unsqueeze(1).to_broadcast([P, Q, PACK]), op=ALU.mult)
+        interleave(turned1, wv[:, I : 2 * I])
+        interleave(turned2, wv[:, 2 * I : 3 * I])
+        wv_codes = sb.tile([P, 3 * P], U32, name="wv_codes", align_bytes=64)
+        wv_scales = sb.tile([P, 3 * P], U8, name="wv_scales", align_bytes=64)
+        quantize(wv_codes[:, 0 : 2 * P], wv_scales[:, 0 : 2 * P], wv[:, 0 : 2 * I])
+        quantize(wv_codes[:, 2 * P : 3 * P], wv_scales[:, 2 * P : 3 * P], wv[:, 2 * I : 3 * I])
+        v3 = sb.tile([P, I], BF16, name="v3", align_bytes=64)
+        interleave(turned3, v3[:])
+        v3_codes = sb.tile([P, P], U32, name="v3_codes", align_bytes=64)
+        v3_scales = sb.tile([P, P], U8, name="v3_scales", align_bytes=64)
+        quantize(v3_codes[:], v3_scales[:], v3[:])
 
-        def product(bank, first, width):
-            cols = slice(first, first + width)
-            nc.tensor.matmul_mx(out=bank, lhsT=w_codes[:].bitcast(FP8X4), lhsT_scale=w_scales[:],
-                                rhs=v_codes[:, cols].bitcast(FP8X4), rhs_scale=v_scales[:, cols], start=True, stop=True)
+        def product(bank, codes, scales):
+            nc.tensor.matmul_mx(out=bank, lhsT=wv_codes[:, 0:P].bitcast(FP8X4), lhsT_scale=wv_scales[:, 0:P],
+                                rhs=codes.bitcast(FP8X4), rhs_scale=scales, start=True, stop=True)
 
-        early_ps = ps.tile([P, 3 * P], F32, name="early_ps")
-        product(early_ps[:, 0 : 2 * P], 0, 2 * P)
-        product(early_ps[:, 2 * P : 3 * P], 2 * P, P)
+        early_ps = ps.tile([P, 3 * P], F32, name="early_ps", tag="a_ps0")
+        product(early_ps[:, 0:P], v0_codes[:], v0_scales[:])
+        product(early_ps[:, P : 3 * P], wv_codes[:, P : 3 * P], wv_scales[:, P : 3 * P])
         early = sb.tile([P, 3 * P], F32, name="early")
         nc.scalar.copy(out=early[:], in_=early_ps[:])
-        nc.sync.dma_start(out=out[:, 0 : 3 * P], in_=early[:])
+        nc.scalar.dma_start(out=out[:, 0 : 3 * P], in_=early[:])
         late_ps = ps.tile([P, P], F32, name="late_ps")
-        product(late_ps[:], 3 * P, P)
+        product(late_ps[:], v3_codes[:], v3_scales[:])
         late = sb.tile([P, P], F32, name="late")
         nc.vector.tensor_copy(out=late[:], in_=late_ps[:])
         nc.sync.dma_start(out=out[:, 3 * P : E], in_=late[:])

@@ -4,7 +4,7 @@ import concourse.mybir as mybir
 from concourse.masks import make_identity
 
 D, E, T, I, Q = 512, 512, 2048, 512, 128
-FLOPS = 2 * D * Q * I * 2 + 2 * I * Q * E
+FLOPS = 2 * (2 * D * Q * I) + 2 * I * Q * E
 
 F32 = mybir.dt.float32
 BF16 = mybir.dt.bfloat16
@@ -18,181 +18,198 @@ ACT = mybir.ActivationFunctionType
 
 P = 128
 PACK = 4
+STRIPE = 16
+HALVES = 2
 CHUNKS = E // P
+MX_ALIGN = 64
+
+COUNT, MINUS_HALF, MINUS_QUARTER, QUARTER, HALF, FIRST_SUM = range(6)
+ROW_MULTIPLES = (I / 2, -0.5, -0.25, 0.25, 0.5)
 
 
 def tile_attend_ttmixedparts_kernel(tc, query, keys_words, keys_scales, share, dquery, slot_factor, vals, offs, out):
     nc = tc.nc
     with ExitStack() as ctx:
         sb = ctx.enter_context(tc.tile_pool(name="sb", bufs=1))
+        last = ctx.enter_context(tc.tile_pool(name="last", bufs=1))
         ps = ctx.enter_context(tc.psum_pool(name="ps", bufs=1))
 
-        offsets = sb.tile([P, I // 16], U16, name="offsets")
+        def column(tile, n):
+            return tile[:, n : n + 1]
+
+        def quantize(codes, scales, rows):
+            nc.vector.quantize_mx(out=codes.bitcast(FP8X4), scales=scales, in_=rows)
+
+        def product(bank, left_codes, left_scales, right_codes, right_scales):
+            nc.tensor.matmul_mx(out=bank, lhsT=left_codes.bitcast(FP8X4), lhsT_scale=left_scales,
+                                rhs=right_codes.bitcast(FP8X4), rhs_scale=right_scales, start=True, stop=True)
+
+        offsets = sb.tile([P, I // STRIPE], U16, name="offsets")
         nc.sync.dma_start(offsets[:], offs)
 
         q_raw = sb.tile([P, PACK, Q], F32, name="q_raw")
-        nc.sync.dma_start(out=q_raw[:], in_=query.rearrange("(p j) q -> p j q", j=PACK))
+        nc.sync.dma_start(out=q_raw[:], in_=query.rearrange("(p t) q -> p t q", t=PACK))
         key_scales = sb.tile([P, T], U8, name="key_scales")
         nc.gpsimd.memset(key_scales[:].bitcast(I32), 0)
-        for quad in range(4):
+        for quad in range(P // 32):
             nc.sync.dma_start(
                 out=key_scales[32 * quad : 32 * quad + 4, :].bitcast(I32),
                 in_=keys_scales[0, 4 * quad : 4 * quad + 4, :].bitcast(I32),
             )
-
         key_words = sb.tile([P, T], U32, name="key_words")
         nc.sync.dma_start(out=key_words[:].bitcast(I32), in_=keys_words[0].rearrange("p n t -> p (n t)").bitcast(I32))
         dq_raw = sb.tile([P, PACK, Q], F32, name="dq_raw")
-        nc.sync.dma_start(out=dq_raw[:], in_=dquery.rearrange("(p j) q -> p j q", j=PACK))
+        nc.sync.dma_start(out=dq_raw[:], in_=dquery.rearrange("(p t) q -> p t q", t=PACK))
         share_col = sb.tile([P, 1], F32, name="share_col")
         nc.sync.dma_start(out=share_col[:], in_=share)
-        os_slots = sb.tile([P, PACK], F32, name="os_slots")
-        nc.sync.dma_start(out=os_slots[:], in_=slot_factor.rearrange("o (p t) -> (o p) t", t=PACK))
+        factor = sb.tile([P, PACK], F32, name="factor")
+        nc.sync.dma_start(out=factor[:], in_=slot_factor.rearrange("o (p t) -> (o p) t", t=PACK))
 
-        val_pool = [sb.tile([P, T], F32, name="val_pool%d" % c, tag="pool%d" % c, align_bytes=64) for c in range(CHUNKS)]
-        nc.sync.dma_start(out=val_pool[0][:], in_=vals[0:P, :])
-        for c in range(1, CHUNKS):
+        val_pool = [sb.tile([P, T], F32, name="val_pool%d" % c, tag="val_pool%d" % c, align_bytes=MX_ALIGN) for c in range(CHUNKS - 1)]
+        last_pool = last.tile([P, T], F32, name="last_pool", offset=0, align_bytes=MX_ALIGN)
+        val_pool.append(last_pool)
+        for c in range(CHUNKS):
             nc.sync.dma_start(out=val_pool[c][:], in_=vals[c * P : (c + 1) * P, :])
 
         ident = sb.tile([P, P], F32, name="ident")
         make_identity(nc, ident[:])
         zero = sb.tile([P, 1], F32, name="zero")
         nc.gpsimd.memset(zero[:], 0.0)
-        multiples = sb.tile([P, 5], F32, name="multiples")
-        for col, value in enumerate((-0.5, -0.25, 0.25, 0.5, I / 2)):
-            nc.gpsimd.memset(multiples[:, col : col + 1], value)
-        mix_s = sb.tile([P, 6], F32, name="mix_s")
-        nc.gpsimd.memset(mix_s[:, 0:1], -1.0)
-        warm = sb.tile([P, 1], F32, name="warm")
-        nc.scalar.activation(out=warm[:], in_=zero[:], func=ACT.Exp)
+        multiples = sb.tile([P, len(ROW_MULTIPLES)], F32, name="multiples")
+        for n, value in enumerate(ROW_MULTIPLES):
+            nc.gpsimd.memset(column(multiples, n), value)
+        row_c = sb.tile([P, FIRST_SUM + 1], F32, name="row_c")
+        nc.gpsimd.memset(column(row_c, 0), -1.0)
 
         rest = sb.tile([P, 1], F32, name="rest")
         nc.scalar.activation(out=rest[:], in_=share_col[:], func=ACT.Copy, scale=-3.0, bias=3.0)
-        mix = sb.tile([P, 5], F32, name="mix")
-        nc.scalar.activation(out=mix[:], in_=multiples[:], func=ACT.Copy, scale=rest[:])
+        row_raw = sb.tile([P, FIRST_SUM + 1], F32, name="row_raw")
+        nc.scalar.activation(out=row_raw[:, 0:FIRST_SUM], in_=multiples[:], func=ACT.Copy, scale=rest[:])
 
-        k_scales = sb.tile([P, I], U8, name="k_scales", align_bytes=64)
+        k_scales = sb.tile([P, I], U8, name="k_scales", align_bytes=MX_ALIGN)
         nc.vector.tensor_copy(out=k_scales[:], in_=key_scales[:].indirect(offsets[:]))
-        q_bf = sb.tile([P, Q, PACK], BF16, name="q_bf", align_bytes=64)
-        nc.vector.tensor_copy(out=q_bf[:], in_=q_raw[:].rearrange("p j q -> p q j"))
-        q_codes = sb.tile([P, Q], U32, name="q_codes", align_bytes=64)
-        q_scales = sb.tile([P, Q], U8, name="q_scales", align_bytes=64)
-        nc.vector.quantize_mx(out=q_codes[:].bitcast(FP8X4), scales=q_scales[:], in_=q_bf[:].rearrange("p q j -> p (q j)"))
-        k_codes = sb.tile([P, I], U32, name="k_codes", align_bytes=64)
-        neg_a = sb.tile([P, PACK, P], F32, name="neg_a")
-        shift_so_far = zero
-        for h in range(2):
-            slots = slice(h * I // 2, (h + 1) * I // 2)
-            nc.vector.tensor_copy(out=k_codes[:, slots], in_=key_words[:].indirect(offsets[:, h * I // 32 : (h + 1) * I // 32]))
-        for h in range(2):
-            slots = slice(h * I // 2, (h + 1) * I // 2)
-            a_ps = ps.tile([P, I // 2], F32, name="a_ps%d" % h)
-            nc.tensor.matmul_mx(out=a_ps[:], lhsT=q_codes[:].bitcast(FP8X4), lhsT_scale=q_scales[:],
-                                rhs=k_codes[:, slots].bitcast(FP8X4), rhs_scale=k_scales[:, slots], start=True, stop=True)
-            shift = sb.tile([P, 1], F32, name="shift%d" % h, tag=("hold0", "shift")[h], align_bytes=64)
-            nc.vector.tensor_scalar(out=neg_a[:, :, h * P // 2 : (h + 1) * P // 2], in0=a_ps[:].rearrange("q (p t) -> q t p", t=PACK),
-                                    scalar1=-1.0, scalar2=shift_so_far[:], op0=ALU.mult, op1=ALU.min, accum_out=shift[:])
-            shift_so_far = shift
+        q_bf = sb.tile([P, Q, PACK], BF16, name="q_bf", align_bytes=MX_ALIGN)
+        nc.vector.tensor_copy(out=q_bf[:], in_=q_raw[:].rearrange("p t q -> p q t"))
+        q_codes = sb.tile([P, Q], U32, name="q_codes", align_bytes=MX_ALIGN)
+        q_scales = sb.tile([P, Q], U8, name="q_scales", align_bytes=MX_ALIGN)
+        quantize(q_codes[:], q_scales[:], q_bf[:].rearrange("p q t -> p (q t)"))
+        k_codes = sb.tile([P, I], U32, name="k_codes", align_bytes=MX_ALIGN)
+        neg_a = sb.tile([P, HALVES, PACK, P // HALVES], F32, name="neg_a")
+        half_slots = [slice(h * I // HALVES, (h + 1) * I // HALVES) for h in range(HALVES)]
+        for slots in half_slots:
+            entries = offsets[:, slots.start // STRIPE : slots.stop // STRIPE]
+            nc.vector.tensor_copy(out=k_codes[:, slots], in_=key_words[:].indirect(entries))
+        first_shift = sb.tile([P, 1], F32, name="first_shift", tag="first_shift", align_bytes=MX_ALIGN)
+        shift = sb.tile([P, 1], F32, name="shift", align_bytes=MX_ALIGN)
+        for h, (so_far, running) in enumerate(((zero, first_shift), (first_shift, shift))):
+            a_ps = ps.tile([P, I // HALVES], F32, name="a_ps%d" % h)
+            product(a_ps[:], q_codes[:], q_scales[:], k_codes[:, half_slots[h]], k_scales[:, half_slots[h]])
+            nc.vector.tensor_scalar(out=neg_a[:, h, :, :], in0=a_ps[:].rearrange("q (s t) -> q t s", t=PACK),
+                                    scalar1=-1.0, scalar2=so_far[:], op0=ALU.mult, op1=ALU.min, accum_out=running[:])
 
-        dq_bf = sb.tile([P, Q, PACK], BF16, name="dq_bf", align_bytes=64)
-        nc.scalar.copy(out=dq_bf[:], in_=dq_raw[:].rearrange("p j q -> p q j"))
-        dq_codes = sb.tile([P, Q], U32, name="dq_codes", align_bytes=64)
-        dq_scales = sb.tile([P, Q], U8, name="dq_scales", align_bytes=64)
-        nc.vector.quantize_mx(out=dq_codes[:].bitcast(FP8X4), scales=dq_scales[:], in_=dq_bf[:].rearrange("p q j -> p (q j)"))
+        dq_bf = sb.tile([P, Q, PACK], BF16, name="dq_bf", align_bytes=MX_ALIGN)
+        nc.scalar.copy(out=dq_bf[:], in_=dq_raw[:].rearrange("p t q -> p q t"))
+        dq_codes = sb.tile([P, Q], U32, name="dq_codes", align_bytes=MX_ALIGN)
+        dq_scales = sb.tile([P, Q], U8, name="dq_scales", align_bytes=MX_ALIGN)
+        quantize(dq_codes[:], dq_scales[:], dq_bf[:].rearrange("p q t -> p (q t)"))
         ta_ps = ps.tile([P, I], F32, name="ta_ps")
-        nc.tensor.matmul_mx(out=ta_ps[:], lhsT=dq_codes[:].bitcast(FP8X4), lhsT_scale=dq_scales[:],
-                            rhs=k_codes[:].bitcast(FP8X4), rhs_scale=k_scales[:], start=True, stop=True)
-        ta_dealt = ta_ps[:].rearrange("q (p t) -> q t p", t=PACK)
+        product(ta_ps[:], dq_codes[:], dq_scales[:], k_codes[:], k_scales[:])
 
-        neg_flat = neg_a[:].rearrange("q t p -> q (t p)")
-        u = sb.tile([P, I], F32, name="u")
-        u_sum = sb.tile([P, 1], F32, name="u_sum")
-        nc.scalar.activation(out=u[:], in_=neg_flat, func=ACT.Tanh, scale=-0.5, accum_out=u_sum[:])
+        u = sb.tile([P, HALVES, PACK, P // HALVES], F32, name="u", tag="u", align_bytes=MX_ALIGN)
+        u_sums = sb.tile([P, HALVES], F32, name="u_sums")
+        for h in range(HALVES):
+            nc.scalar.activation(out=u[:, h, :, :], in_=neg_a[:, h, :, :], func=ACT.Tanh, scale=-0.5, accum_out=column(u_sums, h))
+        nc.scalar.activation(out=column(row_raw, FIRST_SUM), in_=column(u_sums, 0), func=ACT.Identity,
+                             scale=column(row_raw, HALF), bias=column(row_raw, COUNT))
         shrink = sb.tile([P, 1], F32, name="shrink")
         nc.scalar.activation(out=shrink[:], in_=shift[:], func=ACT.Exp)
-        e = sb.tile([P, I], F32, name="e", tag="hold5", align_bytes=64)
-        e_sum = sb.tile([P, 1], F32, name="e_sum")
-        nc.scalar.activation(out=e[:], in_=neg_flat, func=ACT.Exp, scale=-1.0, bias=shift[:], accum_out=e_sum[:])
-        nc.scalar.activation(out=mix_s[:, 1:6], in_=mix[:], func=ACT.Copy, scale=shrink[:])
-        s_sum = sb.tile([P, 1], F32, name="s_sum")
-        nc.scalar.activation(out=s_sum[:], in_=u_sum[:], func=ACT.Identity, scale=mix_s[:, 4:5], bias=mix_s[:, 5:6])
+        exp_a = sb.tile([P, I], F32, name="exp_a")
+        exp_sum = sb.tile([P, 1], F32, name="exp_sum")
+        nc.scalar.activation(out=exp_a[:].rearrange("q (t h s) -> q t h s", t=PACK, h=HALVES), in_=neg_a[:].rearrange("q h t s -> q t h s"),
+                             func=ACT.Exp, scale=-1.0, bias=shift[:], accum_out=exp_sum[:])
+        nc.scalar.activation(out=row_c[:, MINUS_HALF:], in_=row_raw[:, MINUS_HALF:], func=ACT.Copy, scale=shrink[:])
+        sigmoid_sum = sb.tile([P, 1], F32, name="sigmoid_sum")
+        nc.scalar.activation(out=sigmoid_sum[:], in_=column(u_sums, 1), func=ACT.Identity,
+                             scale=column(row_c, HALF), bias=column(row_c, FIRST_SUM))
         z = sb.tile([P, 1], F32, name="z")
-        nc.scalar.activation(out=z[:], in_=e_sum[:], func=ACT.Identity, scale=share_col[:], bias=s_sum[:])
+        nc.scalar.activation(out=z[:], in_=exp_sum[:], func=ACT.Identity, scale=share_col[:], bias=sigmoid_sum[:])
 
-        def gather_values(c):
-            picked = sb.tile([P, I], BF16, name="picked%d" % c, tag=("hold0", "hold1", "hold3", "pool2")[c], align_bytes=64)
+        def gather_values(c, takes_over, turned):
+            picked = sb.tile([P, I], BF16, name="picked%d" % c, tag=takes_over, align_bytes=MX_ALIGN)
             nc.vector.tensor_copy(out=picked[:], in_=val_pool[c][:].indirect(offsets[:]))
             words = picked[:].bitcast(F32)
-            turned = ps.tile([P, 2, P], F32, name="turned", tag="turned", bufs=3)
-            for h in range(2):
-                nc.tensor.transpose(turned[:, h, :], words[:, h : I // 2 : 2], ident[:])
-            return turned
+            for w in range(2):
+                nc.tensor.transpose(turned[:, w, :], words[:, w : I // 2 : 2], ident[:])
 
         def interleave(turned, rows):
-            nc.scalar.copy(out=rows.bitcast(F32).rearrange("p (e h) -> p e h", h=2), in_=turned[:].rearrange("p h e -> p e h"))
+            nc.scalar.copy(out=rows.bitcast(F32).rearrange("p (c e w) -> p c e w", e=P, w=2), in_=turned.rearrange("p c w e -> p c e w"))
 
-        def quantize(codes, scales, rows):
-            nc.vector.quantize_mx(out=codes.bitcast(FP8X4), scales=scales, in_=rows)
-
-        turned0 = gather_values(0)
-        u_sq = sb.tile([P, I], F32, name="u_sq", tag="pool0", align_bytes=64)
-        nc.vector.tensor_tensor(out=u_sq[:], in0=u[:], in1=u[:], op=ALU.mult)
-        base = sb.tile([P, I], F32, name="base")
-        nc.vector.tensor_scalar(out=base[:], in0=e[:], scalar1=share_col[:], scalar2=mix_s[:, 3:4], op0=ALU.mult, op1=ALU.add)
-        z_inv = sb.tile([P, 1], F32, name="z_inv", tag="hold3", align_bytes=64)
+        turned0 = ps.tile([P, 1, 2, P], F32, name="turned0", tag="turned")
+        gather_values(0, "first_shift", turned0[:, 0, :, :])
+        pair = sb.tile([P, 2 * I], F32, name="pair", tag="val_pool0", align_bytes=MX_ALIGN)
+        u_sq, base = pair[:, 0:I], pair[:, I : 2 * I]
+        u_dealt = u[:].rearrange("q h t s -> q t h s")
+        nc.vector.tensor_tensor(out=u_sq.rearrange("q (t h s) -> q t h s", t=PACK, h=HALVES), in0=u_dealt, in1=u_dealt, op=ALU.mult)
+        nc.vector.tensor_scalar(out=base, in0=exp_a[:], scalar1=share_col[:], scalar2=column(row_c, QUARTER), op0=ALU.mult, op1=ALU.add)
+        slope = sb.tile([P, I], F32, name="slope", tag="slope", align_bytes=MX_ALIGN)
+        nc.vector.scalar_tensor_tensor(out=slope[:], in0=u_sq, scalar=column(row_c, MINUS_QUARTER), in1=base, op0=ALU.mult, op1=ALU.add)
+        z_inv = sb.tile([P, 1], F32, name="z_inv", tag="z_inv", align_bytes=MX_ALIGN)
         nc.vector.reciprocal(out=z_inv[:], in_=z[:])
-        slope = sb.tile([P, I], F32, name="slope", tag="hold1", align_bytes=64)
-        nc.vector.scalar_tensor_tensor(out=slope[:], in0=u_sq[:], scalar=mix_s[:, 2:3], in1=base[:], op0=ALU.mult, op1=ALU.add)
-        v0 = sb.tile([P, I], BF16, name="v0", tag="hold5", align_bytes=64)
-        interleave(turned0, v0[:])
-        per_z = sb.tile([P, 3], F32, name="per_z")
-        nc.scalar.activation(out=per_z[:], in_=mix_s[:, 0:3], func=ACT.Copy, scale=z_inv[:])
-        terms = [sb.tile([P, PACK, P], F32, name="term%d" % n) for n in range(3)]
+        per_z = sb.tile([P, QUARTER], F32, name="per_z")
+        nc.scalar.activation(out=per_z[:], in_=row_c[:, 0:QUARTER], func=ACT.Copy, scale=z_inv[:])
+
+        tangent = sb.tile([P, PACK, P], F32, name="tangent", align_bytes=MX_ALIGN)
+        base_term = sb.tile([P, PACK, P], F32, name="base_term", align_bytes=MX_ALIGN)
+        u_term = sb.tile([P, PACK, P], F32, name="u_term", align_bytes=MX_ALIGN)
         ratio = sb.tile([P, 1], F32, name="ratio")
-        nc.vector.scalar_tensor_tensor(out=terms[0][:], in0=slope[:].rearrange("q (t p) -> q t p", t=PACK), scalar=z_inv[:], in1=ta_dealt,
-                                       op0=ALU.mult, op1=ALU.mult, accum_out=ratio[:])
-        pull = sb.tile([P, 3], F32, name="pull")
+        nc.vector.scalar_tensor_tensor(out=tangent[:], in0=slope[:].rearrange("q (t p) -> q t p", t=PACK), scalar=z_inv[:],
+                                       in1=ta_ps[:].rearrange("q (p t) -> q t p", t=PACK), op0=ALU.mult, op1=ALU.mult, accum_out=ratio[:])
+        pull = sb.tile([P, QUARTER], F32, name="pull")
         nc.scalar.activation(out=pull[:], in_=per_z[:], func=ACT.Copy, scale=ratio[:])
-        nc.scalar.activation(out=terms[1][:].rearrange("q t p -> q (t p)"), in_=base[:], func=ACT.Copy, scale=pull[:, 0:1])
-        nc.scalar.activation(out=terms[2][:].rearrange("q t p -> q (t p)"), in_=u[:], func=ACT.Identity, scale=pull[:, 1:2], bias=pull[:, 2:3])
+        nc.scalar.activation(out=base_term[:].rearrange("q t p -> q (t p)"), in_=base, func=ACT.Copy, scale=column(pull, 0))
+        nc.scalar.activation(out=u_term[:].rearrange("q t (h s) -> q t h s", h=HALVES), in_=u_dealt, func=ACT.Identity,
+                             scale=column(pull, MINUS_HALF), bias=column(pull, MINUS_QUARTER))
         tw_ps = ps.tile([P, PACK, Q], F32, name="tw_ps")
+        terms = (tangent, base_term, u_term)
         for n, term in enumerate(terms):
             for t in range(PACK):
                 nc.tensor.matmul(tw_ps[:, t, :], lhsT=term[:, t, :], rhs=ident[:], is_transpose=True,
                                  start=(n == 0 and t == 0), stop=(n == len(terms) - 1 and t == PACK - 1))
-        turned1 = gather_values(1)
-        turned2 = gather_values(2)
-        v0_codes = sb.tile([P, P], U32, name="v0_codes", tag="pool1", align_bytes=64)
-        v0_scales = sb.tile([P, P], U8, name="v0_scales", align_bytes=64)
-        quantize(v0_codes[:], v0_scales[:], v0[:])
-        turned3 = gather_values(3)
-        wv = sb.tile([P, 3 * I], BF16, name="wv", tag="pool3", align_bytes=64)
-        nc.vector.tensor_tensor(out=wv[:, 0:I].rearrange("p (q t) -> p q t", t=PACK), in0=tw_ps[:].rearrange("p t q -> p q t"),
-                                in1=os_slots[:].unsqueeze(1).to_broadcast([P, Q, PACK]), op=ALU.mult)
-        interleave(turned1, wv[:, I : 2 * I])
-        interleave(turned2, wv[:, 2 * I : 3 * I])
-        wv_codes = sb.tile([P, 3 * P], U32, name="wv_codes", align_bytes=64)
-        wv_scales = sb.tile([P, 3 * P], U8, name="wv_scales", align_bytes=64)
-        quantize(wv_codes[:, 0 : 2 * P], wv_scales[:, 0 : 2 * P], wv[:, 0 : 2 * I])
-        quantize(wv_codes[:, 2 * P : 3 * P], wv_scales[:, 2 * P : 3 * P], wv[:, 2 * I : 3 * I])
-        v3 = sb.tile([P, I], BF16, name="v3", align_bytes=64)
-        interleave(turned3, v3[:])
-        v3_codes = sb.tile([P, P], U32, name="v3_codes", align_bytes=64)
-        v3_scales = sb.tile([P, P], U8, name="v3_scales", align_bytes=64)
-        quantize(v3_codes[:], v3_scales[:], v3[:])
 
-        def product(bank, codes, scales):
-            nc.tensor.matmul_mx(out=bank, lhsT=wv_codes[:, 0:P].bitcast(FP8X4), lhsT_scale=wv_scales[:, 0:P],
-                                rhs=codes.bitcast(FP8X4), rhs_scale=scales, start=True, stop=True)
+        v0 = sb.tile([P, I], BF16, name="v0", tag="u", align_bytes=MX_ALIGN)
+        interleave(turned0[:], v0[:])
+        turned12 = ps.tile([P, 2, 2, P], F32, name="turned12", tag="turned")
+        gather_values(1, "slope", turned12[:, 0, :, :])
+        gather_values(2, "z_inv", turned12[:, 1, :, :])
+        v12 = sb.tile([P, 2 * I], BF16, name="v12", align_bytes=MX_ALIGN)
+        interleave(turned12[:], v12[:])
+        turned3 = ps.tile([P, 1, 2, P], F32, name="turned3")
+        gather_values(3, "val_pool0", turned3[:, 0, :, :])
+        v3 = sb.tile([P, I], BF16, name="v3", align_bytes=MX_ALIGN)
+        interleave(turned3[:], v3[:])
 
-        early_ps = ps.tile([P, 3 * P], F32, name="early_ps", tag="a_ps0")
-        product(early_ps[:, 0:P], v0_codes[:], v0_scales[:])
-        product(early_ps[:, P : 3 * P], wv_codes[:, P : 3 * P], wv_scales[:, P : 3 * P])
-        early = sb.tile([P, 3 * P], F32, name="early")
+        w_bf = last.tile([P, Q, PACK], BF16, name="w_bf", offset=0, align_bytes=MX_ALIGN)
+        nc.vector.tensor_tensor(out=w_bf[:], in0=tw_ps[:].rearrange("p t q -> p q t"),
+                                in1=factor[:].unsqueeze(1).to_broadcast([P, Q, PACK]), op=ALU.mult)
+        w_bytes = 2 * Q * PACK
+        v_codes = last.tile([P, E], U32, name="v_codes", offset=w_bytes, align_bytes=MX_ALIGN)
+        v_scales = sb.tile([P, E], U8, name="v_scales", align_bytes=MX_ALIGN)
+        w_codes = sb.tile([P, Q], U32, name="w_codes", align_bytes=MX_ALIGN)
+        w_scales = sb.tile([P, Q], U8, name="w_scales", align_bytes=MX_ALIGN)
+        chunk0, chunks12, chunk3 = slice(0, P), slice(P, 3 * P), slice(3 * P, E)
+        quantize(v_codes[:, chunks12], v_scales[:, chunks12], v12[:])
+        quantize(w_codes[:], w_scales[:], w_bf[:].rearrange("p q t -> p (q t)"))
+        quantize(v_codes[:, chunk0], v_scales[:, chunk0], v0[:])
+        quantize(v_codes[:, chunk3], v_scales[:, chunk3], v3[:])
+
+        early_ps = ps.tile([P, chunk3.start], F32, name="early_ps")
+        for cols in (chunks12, chunk0):
+            product(early_ps[:, cols], w_codes[:], w_scales[:], v_codes[:, cols], v_scales[:, cols])
+        early = sb.tile([P, chunk3.start], F32, name="early")
         nc.scalar.copy(out=early[:], in_=early_ps[:])
-        nc.scalar.dma_start(out=out[:, 0 : 3 * P], in_=early[:])
+        nc.scalar.dma_start(out=out[:, 0 : chunk3.start], in_=early[:])
         late_ps = ps.tile([P, P], F32, name="late_ps")
-        product(late_ps[:], v3_codes[:], v3_scales[:])
+        product(late_ps[:], w_codes[:], w_scales[:], v_codes[:, chunk3], v_scales[:, chunk3])
         late = sb.tile([P, P], F32, name="late")
         nc.vector.tensor_copy(out=late[:], in_=late_ps[:])
-        nc.sync.dma_start(out=out[:, 3 * P : E], in_=late[:])
+        nc.sync.dma_start(out=out[:, chunk3], in_=late[:])

from contextlib import ExitStack

import concourse.mybir as mybir
from concourse.masks import make_identity

D, E, T, I, Q = 512, 512, 2048, 512, 128
FLOPS = 2 * (2 * D * Q * I) + 2 * I * Q * E

F32 = mybir.dt.float32
BF16 = mybir.dt.bfloat16
I32 = mybir.dt.int32
U32 = mybir.dt.uint32
U16 = mybir.dt.uint16
U8 = mybir.dt.uint8
FP8X4 = mybir.dt.float8_e4m3fn_x4
ALU = mybir.AluOpType
ACT = mybir.ActivationFunctionType

P = 128
PACK = 4
STRIPE = 16
HALVES = 2
CHUNKS = E // P
MX_ALIGN = 64

COUNT, MINUS_HALF, MINUS_QUARTER, QUARTER, HALF, FIRST_SUM = range(6)
ROW_MULTIPLES = (I / 2, -0.5, -0.25, 0.25, 0.5)


def tile_attend_ttmixedparts_kernel(tc, query, keys_words, keys_scales, share, dquery, slot_factor, vals, offs, out):
    nc = tc.nc
    with ExitStack() as ctx:
        sb = ctx.enter_context(tc.tile_pool(name="sb", bufs=1))
        last = ctx.enter_context(tc.tile_pool(name="last", bufs=1))
        ps = ctx.enter_context(tc.psum_pool(name="ps", bufs=1))

        def column(tile, n):
            return tile[:, n : n + 1]

        def quantize(codes, scales, rows):
            nc.vector.quantize_mx(out=codes.bitcast(FP8X4), scales=scales, in_=rows)

        def product(bank, left_codes, left_scales, right_codes, right_scales):
            nc.tensor.matmul_mx(out=bank, lhsT=left_codes.bitcast(FP8X4), lhsT_scale=left_scales,
                                rhs=right_codes.bitcast(FP8X4), rhs_scale=right_scales, start=True, stop=True)

        offsets = sb.tile([P, I // STRIPE], U16, name="offsets")
        nc.sync.dma_start(offsets[:], offs)

        q_raw = sb.tile([P, PACK, Q], F32, name="q_raw")
        nc.sync.dma_start(out=q_raw[:], in_=query.rearrange("(p t) q -> p t q", t=PACK))
        key_scales = sb.tile([P, T], U8, name="key_scales")
        nc.gpsimd.memset(key_scales[:].bitcast(I32), 0)
        for quad in range(P // 32):
            nc.sync.dma_start(
                out=key_scales[32 * quad : 32 * quad + 4, :].bitcast(I32),
                in_=keys_scales[0, 4 * quad : 4 * quad + 4, :].bitcast(I32),
            )
        key_words = sb.tile([P, T], U32, name="key_words")
        nc.sync.dma_start(out=key_words[:].bitcast(I32), in_=keys_words[0].rearrange("p n t -> p (n t)").bitcast(I32))
        dq_raw = sb.tile([P, PACK, Q], F32, name="dq_raw")
        nc.sync.dma_start(out=dq_raw[:], in_=dquery.rearrange("(p t) q -> p t q", t=PACK))
        share_col = sb.tile([P, 1], F32, name="share_col")
        nc.sync.dma_start(out=share_col[:], in_=share)
        factor = sb.tile([P, PACK], F32, name="factor")
        nc.sync.dma_start(out=factor[:], in_=slot_factor.rearrange("o (p t) -> (o p) t", t=PACK))

        val_pool = [sb.tile([P, T], F32, name="val_pool%d" % c, tag="val_pool%d" % c, align_bytes=MX_ALIGN) for c in range(CHUNKS - 1)]
        last_pool = last.tile([P, T], F32, name="last_pool", offset=0, align_bytes=MX_ALIGN)
        val_pool.append(last_pool)
        for c in range(CHUNKS):
            nc.sync.dma_start(out=val_pool[c][:], in_=vals[c * P : (c + 1) * P, :])

        ident = sb.tile([P, P], F32, name="ident")
        make_identity(nc, ident[:])
        zero = sb.tile([P, 1], F32, name="zero")
        nc.gpsimd.memset(zero[:], 0.0)
        multiples = sb.tile([P, len(ROW_MULTIPLES)], F32, name="multiples")
        for n, value in enumerate(ROW_MULTIPLES):
            nc.gpsimd.memset(column(multiples, n), value)
        row_c = sb.tile([P, FIRST_SUM + 1], F32, name="row_c")
        nc.gpsimd.memset(column(row_c, 0), -1.0)

        rest = sb.tile([P, 1], F32, name="rest")
        nc.scalar.activation(out=rest[:], in_=share_col[:], func=ACT.Copy, scale=-3.0, bias=3.0)
        row_raw = sb.tile([P, FIRST_SUM + 1], F32, name="row_raw")
        nc.scalar.activation(out=row_raw[:, 0:FIRST_SUM], in_=multiples[:], func=ACT.Copy, scale=rest[:])

        k_scales = sb.tile([P, I], U8, name="k_scales", align_bytes=MX_ALIGN)
        nc.vector.tensor_copy(out=k_scales[:], in_=key_scales[:].indirect(offsets[:]))
        q_bf = sb.tile([P, Q, PACK], BF16, name="q_bf", align_bytes=MX_ALIGN)
        nc.vector.tensor_copy(out=q_bf[:], in_=q_raw[:].rearrange("p t q -> p q t"))
        q_codes = sb.tile([P, Q], U32, name="q_codes", align_bytes=MX_ALIGN)
        q_scales = sb.tile([P, Q], U8, name="q_scales", align_bytes=MX_ALIGN)
        quantize(q_codes[:], q_scales[:], q_bf[:].rearrange("p q t -> p (q t)"))
        k_codes = sb.tile([P, I], U32, name="k_codes", align_bytes=MX_ALIGN)
        neg_a = sb.tile([P, HALVES, PACK, P // HALVES], F32, name="neg_a")
        half_slots = [slice(h * I // HALVES, (h + 1) * I // HALVES) for h in range(HALVES)]
        for slots in half_slots:
            entries = offsets[:, slots.start // STRIPE : slots.stop // STRIPE]
            nc.vector.tensor_copy(out=k_codes[:, slots], in_=key_words[:].indirect(entries))
        first_shift = sb.tile([P, 1], F32, name="first_shift", tag="first_shift", align_bytes=MX_ALIGN)
        shift = sb.tile([P, 1], F32, name="shift", align_bytes=MX_ALIGN)
        for h, (so_far, running) in enumerate(((zero, first_shift), (first_shift, shift))):
            a_ps = ps.tile([P, I // HALVES], F32, name="a_ps%d" % h)
            product(a_ps[:], q_codes[:], q_scales[:], k_codes[:, half_slots[h]], k_scales[:, half_slots[h]])
            nc.vector.tensor_scalar(out=neg_a[:, h, :, :], in0=a_ps[:].rearrange("q (s t) -> q t s", t=PACK),
                                    scalar1=-1.0, scalar2=so_far[:], op0=ALU.mult, op1=ALU.min, accum_out=running[:])

        dq_bf = sb.tile([P, Q, PACK], BF16, name="dq_bf", align_bytes=MX_ALIGN)
        nc.scalar.copy(out=dq_bf[:], in_=dq_raw[:].rearrange("p t q -> p q t"))
        dq_codes = sb.tile([P, Q], U32, name="dq_codes", align_bytes=MX_ALIGN)
        dq_scales = sb.tile([P, Q], U8, name="dq_scales", align_bytes=MX_ALIGN)
        quantize(dq_codes[:], dq_scales[:], dq_bf[:].rearrange("p q t -> p (q t)"))
        ta_ps = ps.tile([P, I], F32, name="ta_ps")
        product(ta_ps[:], dq_codes[:], dq_scales[:], k_codes[:], k_scales[:])

        u = sb.tile([P, HALVES, PACK, P // HALVES], F32, name="u", tag="u", align_bytes=MX_ALIGN)
        u_sums = sb.tile([P, HALVES], F32, name="u_sums")
        for h in range(HALVES):
            nc.scalar.activation(out=u[:, h, :, :], in_=neg_a[:, h, :, :], func=ACT.Tanh, scale=-0.5, accum_out=column(u_sums, h))
        nc.scalar.activation(out=column(row_raw, FIRST_SUM), in_=column(u_sums, 0), func=ACT.Identity,
                             scale=column(row_raw, HALF), bias=column(row_raw, COUNT))
        shrink = sb.tile([P, 1], F32, name="shrink")
        nc.scalar.activation(out=shrink[:], in_=shift[:], func=ACT.Exp)
        exp_a = sb.tile([P, I], F32, name="exp_a")
        exp_sum = sb.tile([P, 1], F32, name="exp_sum")
        nc.scalar.activation(out=exp_a[:].rearrange("q (t h s) -> q t h s", t=PACK, h=HALVES), in_=neg_a[:].rearrange("q h t s -> q t h s"),
                             func=ACT.Exp, scale=-1.0, bias=shift[:], accum_out=exp_sum[:])
        nc.scalar.activation(out=row_c[:, MINUS_HALF:], in_=row_raw[:, MINUS_HALF:], func=ACT.Copy, scale=shrink[:])
        sigmoid_sum = sb.tile([P, 1], F32, name="sigmoid_sum")
        nc.scalar.activation(out=sigmoid_sum[:], in_=column(u_sums, 1), func=ACT.Identity,
                             scale=column(row_c, HALF), bias=column(row_c, FIRST_SUM))
        z = sb.tile([P, 1], F32, name="z")
        nc.scalar.activation(out=z[:], in_=exp_sum[:], func=ACT.Identity, scale=share_col[:], bias=sigmoid_sum[:])

        def gather_values(c, takes_over, turned):
            picked = sb.tile([P, I], BF16, name="picked%d" % c, tag=takes_over, align_bytes=MX_ALIGN)
            nc.vector.tensor_copy(out=picked[:], in_=val_pool[c][:].indirect(offsets[:]))
            words = picked[:].bitcast(F32)
            for w in range(2):
                nc.tensor.transpose(turned[:, w, :], words[:, w : I // 2 : 2], ident[:])

        def interleave(turned, rows):
            nc.scalar.copy(out=rows.bitcast(F32).rearrange("p (c e w) -> p c e w", e=P, w=2), in_=turned.rearrange("p c w e -> p c e w"))

        turned0 = ps.tile([P, 1, 2, P], F32, name="turned0", tag="turned")
        gather_values(0, "first_shift", turned0[:, 0, :, :])
        pair = sb.tile([P, 2 * I], F32, name="pair", tag="val_pool0", align_bytes=MX_ALIGN)
        u_sq, base = pair[:, 0:I], pair[:, I : 2 * I]
        u_dealt = u[:].rearrange("q h t s -> q t h s")
        nc.vector.tensor_tensor(out=u_sq.rearrange("q (t h s) -> q t h s", t=PACK, h=HALVES), in0=u_dealt, in1=u_dealt, op=ALU.mult)
        nc.vector.tensor_scalar(out=base, in0=exp_a[:], scalar1=share_col[:], scalar2=column(row_c, QUARTER), op0=ALU.mult, op1=ALU.add)
        slope = sb.tile([P, I], F32, name="slope", tag="slope", align_bytes=MX_ALIGN)
        nc.vector.scalar_tensor_tensor(out=slope[:], in0=u_sq, scalar=column(row_c, MINUS_QUARTER), in1=base, op0=ALU.mult, op1=ALU.add)
        z_inv = sb.tile([P, 1], F32, name="z_inv", tag="z_inv", align_bytes=MX_ALIGN)
        nc.vector.reciprocal(out=z_inv[:], in_=z[:])
        per_z = sb.tile([P, QUARTER], F32, name="per_z")
        nc.scalar.activation(out=per_z[:], in_=row_c[:, 0:QUARTER], func=ACT.Copy, scale=z_inv[:])

        tangent = sb.tile([P, PACK, P], F32, name="tangent", align_bytes=MX_ALIGN)
        base_term = sb.tile([P, PACK, P], F32, name="base_term", align_bytes=MX_ALIGN)
        u_term = sb.tile([P, PACK, P], F32, name="u_term", align_bytes=MX_ALIGN)
        ratio = sb.tile([P, 1], F32, name="ratio")
        nc.vector.scalar_tensor_tensor(out=tangent[:], in0=slope[:].rearrange("q (t p) -> q t p", t=PACK), scalar=z_inv[:],
                                       in1=ta_ps[:].rearrange("q (p t) -> q t p", t=PACK), op0=ALU.mult, op1=ALU.mult, accum_out=ratio[:])
        pull = sb.tile([P, QUARTER], F32, name="pull")
        nc.scalar.activation(out=pull[:], in_=per_z[:], func=ACT.Copy, scale=ratio[:])
        nc.scalar.activation(out=base_term[:].rearrange("q t p -> q (t p)"), in_=base, func=ACT.Copy, scale=column(pull, 0))
        nc.scalar.activation(out=u_term[:].rearrange("q t (h s) -> q t h s", h=HALVES), in_=u_dealt, func=ACT.Identity,
                             scale=column(pull, MINUS_HALF), bias=column(pull, MINUS_QUARTER))
        tw_ps = ps.tile([P, PACK, Q], F32, name="tw_ps")
        terms = (tangent, base_term, u_term)
        for n, term in enumerate(terms):
            for t in range(PACK):
                nc.tensor.matmul(tw_ps[:, t, :], lhsT=term[:, t, :], rhs=ident[:], is_transpose=True,
                                 start=(n == 0 and t == 0), stop=(n == len(terms) - 1 and t == PACK - 1))

        v0 = sb.tile([P, I], BF16, name="v0", tag="u", align_bytes=MX_ALIGN)
        interleave(turned0[:], v0[:])
        turned12 = ps.tile([P, 2, 2, P], F32, name="turned12", tag="turned")
        gather_values(1, "slope", turned12[:, 0, :, :])
        gather_values(2, "z_inv", turned12[:, 1, :, :])
        v12 = sb.tile([P, 2 * I], BF16, name="v12", align_bytes=MX_ALIGN)
        interleave(turned12[:], v12[:])
        turned3 = ps.tile([P, 1, 2, P], F32, name="turned3")
        gather_values(3, "val_pool0", turned3[:, 0, :, :])
        v3 = sb.tile([P, I], BF16, name="v3", align_bytes=MX_ALIGN)
        interleave(turned3[:], v3[:])

        w_bf = last.tile([P, Q, PACK], BF16, name="w_bf", offset=0, align_bytes=MX_ALIGN)
        nc.vector.tensor_tensor(out=w_bf[:], in0=tw_ps[:].rearrange("p t q -> p q t"),
                                in1=factor[:].unsqueeze(1).to_broadcast([P, Q, PACK]), op=ALU.mult)
        w_bytes = 2 * Q * PACK
        v_codes = last.tile([P, E], U32, name="v_codes", offset=w_bytes, align_bytes=MX_ALIGN)
        v_scales = sb.tile([P, E], U8, name="v_scales", align_bytes=MX_ALIGN)
        w_codes = sb.tile([P, Q], U32, name="w_codes", align_bytes=MX_ALIGN)
        w_scales = sb.tile([P, Q], U8, name="w_scales", align_bytes=MX_ALIGN)
        chunk0, chunks12, chunk3 = slice(0, P), slice(P, 3 * P), slice(3 * P, E)
        quantize(v_codes[:, chunks12], v_scales[:, chunks12], v12[:])
        quantize(w_codes[:], w_scales[:], w_bf[:].rearrange("p q t -> p (q t)"))
        quantize(v_codes[:, chunk0], v_scales[:, chunk0], v0[:])
        quantize(v_codes[:, chunk3], v_scales[:, chunk3], v3[:])

        early_ps = ps.tile([P, chunk3.start], F32, name="early_ps")
        for cols in (chunks12, chunk0):
            product(early_ps[:, cols], w_codes[:], w_scales[:], v_codes[:, cols], v_scales[:, cols])
        early = sb.tile([P, chunk3.start], F32, name="early")
        nc.scalar.copy(out=early[:], in_=early_ps[:])
        nc.scalar.dma_start(out=out[:, 0 : chunk3.start], in_=early[:])
        late_ps = ps.tile([P, P], F32, name="late_ps")
        product(late_ps[:], w_codes[:], w_scales[:], v_codes[:, chunk3], v_scales[:, chunk3])
        late = sb.tile([P, P], F32, name="late")
        nc.vector.tensor_copy(out=late[:], in_=late_ps[:])
        nc.sync.dma_start(out=out[:, chunk3], in_=late[:])
